import numpy as np
import ml_dtypes


def mxq(x, axis, fmt="e4m3"):
    dtype, down = {"e4m3": (ml_dtypes.float8_e4m3fn, 7), "e5m2": (ml_dtypes.float8_e5m2, 14)}[fmt]
    v = np.moveaxis(np.asarray(x, np.float32).astype(ml_dtypes.bfloat16).astype(np.float64), axis, -1)
    blocks = v.reshape(v.shape[:-1] + (-1, 32))
    amax = np.abs(blocks).max(-1, keepdims=True)
    byte = np.maximum(np.where(amax > 0, np.frexp(amax)[1] - 1 + 127, 0) - down, 1)
    scale = np.exp2(byte - 127.0)
    codes = (blocks / scale).astype(np.float32).astype(dtype).astype(np.float64)
    return np.moveaxis((codes * scale).reshape(v.shape), -1, axis)


WIDE = False


def mx_kscale(k):
    if not WIDE:
        return np.ones(k)
    levels = np.array([10, -10, 5, -5, 0])
    if k % 512:
        return np.exp2(np.random.permutation(np.resize(levels, k // 32))).repeat(32)
    a = np.empty((k // 512, 16))
    for p in range(k // 512):
        a[p, :8] = np.random.permutation(np.resize(levels, 8))
        for g in range(8):
            far = levels[np.abs(levels - a[p, g]) >= 10]
            a[p, g + 8] = far[np.random.randint(len(far))]
    return np.exp2(a.ravel()).repeat(32)


def f64(x):
    return np.asarray(x).astype(np.float64)


def striped(idx):
    return np.tile(idx.reshape(-1, 16).T, (8, 1)).astype(np.uint16)


def unstriped(offs):
    return offs[:16].T.reshape(-1).astype(np.int64)


E2M1 = np.array([0.0, 0.5, 1.0, 1.5, 2.0, 3.0, 4.0, 6.0, -0.0, -0.5, -1.0, -1.5, -2.0, -3.0, -4.0, -6.0])


def pack_weight(w, fmt):
    k, n = w.shape
    w = f64(np.asarray(w, np.float32).astype(ml_dtypes.bfloat16)).reshape(k // 32, 32, n)
    amax = np.abs(w).max(1)
    if fmt == "e4m3":
        byte = np.frexp(amax)[1] - 1 + 127 - 7
    else:
        mant, ex = np.frexp(amax / 6.0)
        byte = np.where(mant > 0.5, ex, ex - 1) + 127
    byte = np.clip(np.where(amax > 0, byte, 1), 1, 254)
    scaled = (w * np.exp2(127.0 - byte)[:, None, :]).reshape(k, n).astype(np.float32)
    by_word = np.ascontiguousarray(scaled.reshape(k // 512, 128, 4, n).transpose(0, 1, 3, 2))
    if fmt == "e4m3":
        words = by_word.astype(ml_dtypes.float8_e4m3fn).view(np.uint8)
    else:
        c = by_word.astype(ml_dtypes.float4_e2m1fn).view(np.uint8) & 0xF
        words = (c[..., 0::2] | (c[..., 1::2] << 4)).reshape(k // 512, 128, 2 * n)
    return np.ascontiguousarray(words), np.ascontiguousarray(byte.astype(np.uint8).reshape(k // 512, 16, n))


def unpack_weight(words, scales, fmt):
    g, _, n = scales.shape
    words = np.ascontiguousarray(words).reshape(g, 128, n, -1)
    if fmt == "e4m3":
        vals = words.view(ml_dtypes.float8_e4m3fn).astype(np.float64)
    else:
        nib = np.empty((g, 128, n, 4), np.uint8)
        nib[..., 0::2] = words & 0xF
        nib[..., 1::2] = words >> 4
        vals = E2M1[nib]
    vals = vals * np.repeat(np.exp2(scales.astype(np.float64) - 127.0), 8, axis=1)[..., None]
    return vals.transpose(0, 1, 3, 2).reshape(g * 512, n)


def silu(v):
    return v / (1.0 + np.exp(-np.maximum(v, -700.0)))


K, T, E, C, N = 512, 1536, 8, 128, 128


def by_expert(wq, xq):
    return np.concatenate([wq[e].T @ xq[:, e * C:(e + 1) * C] for e in range(E)], axis=1)


def setup_inputs():
    n = np.random.standard_normal
    s = mx_kscale(K)[:, None]
    w = [pack_weight(m, "e2m1") for m in n((E, K, N)) / np.sqrt(K) / s[None]]
    return {
        "xT": (n((K, T)) * s).astype(np.float32),
        "xr": n((N, T)).astype(np.float32),
        "w_words": np.stack([m[0] for m in w]),
        "w_scales": np.stack([m[1] for m in w]),
        "b": (0.3 * n((N, E))).astype(np.float32),
        "gate": np.tile(np.random.uniform(0.2, 1.0, E * C), (N, 1)).astype(np.float32),
        "offs": striped(np.random.permutation(T)[:E * C]),
    }


def reference(xT, xr, w_words, w_scales, b, gate, offs):
    idx = unstriped(offs)
    w = np.stack([unpack_weight(w_words[e], w_scales[e], "e2m1") for e in range(E)])
    xq = mxq(f64(xT)[:, idx], 0, "e4m3")
    y = by_expert(w, xq)
    y = silu(y + np.repeat(f64(b), C, axis=1))
    out = f64(xr).copy()
    out[:, idx] += f64(gate) * y
    return out

@@ -1,0 +1,118 @@
+import concourse.mybir as mybir
+
+K, T, E, C, N = 512, 1536, 8, 128, 128
+FLOPS = 2 * K * N * E * C
+
+F32 = mybir.dt.float32
+BF16 = mybir.dt.bfloat16
+I32 = mybir.dt.int32
+U32 = mybir.dt.uint32
+U16 = mybir.dt.uint16
+U8 = mybir.dt.uint8
+FP8X4 = mybir.dt.float8_e4m3fn_x4
+FP4X4 = mybir.dt.float4_e2m1fn_x4
+MULT, ADD = mybir.AluOpType.mult, mybir.AluOpType.add
+SILU = mybir.ActivationFunctionType.Silu
+COPY = mybir.ActivationFunctionType.Copy
+
+P = 128
+PACK = 4
+
+CHUNKS = ((0, 512, 320), (512, 512, 320), (1024, 256, 160), (1280, 256, 160))
+GROUPS = ((0, 1, 2, 3), (4, 5, 6, 7))
+STORES = ((0, 512), (512, 1024), (1024, 1280), (1280, 1536))
+
+
+def interleaved(grouped, a, b):
+    return grouped[:, a:b, :].rearrange("p (c i) t -> p c t i", i=4)
+
+
+def by_rows(raw, a, b):
+    return raw[:, :, a:b].rearrange("p t (c i) -> p c t i", i=4)
+
+
+def tile_moe_res_lin_silu_kernel(tc, xT, xr, w_words, w_scales, b, gate, offs, out):
+    nc = tc.nc
+    with (
+        tc.tile_pool(name="keep", bufs=1) as keep,
+        tc.psum_pool(name="psum", bufs=1) as psum,
+    ):
+        offsets = keep.tile([P, E * C // 16], U16, name="offsets")
+        words = keep.tile([P, T], U32, name="words", align_bytes=64)
+        scales = keep.tile([P, T], U8, name="scales", align_bytes=64)
+        w_codes = keep.tile([P, E, 2 * N], U8, name="w_codes", align_bytes=64)
+        w_bytes = keep.tile([P, E, N], U8, name="w_bytes", align_bytes=64)
+        bias = keep.tile([P, E], F32, name="bias")
+        gates = keep.tile([P, E * C], F32, name="gates")
+        residual = keep.tile([P, T], F32, name="residual")
+        placed = keep.tile([P, T], F32, name="placed")
+        warm = keep.tile([P, 1], F32, name="warm")
+        warmed = keep.tile([P, 1], F32, name="warmed")
+
+        tokens = xT.rearrange("(p j) t -> p j t", j=PACK)
+        raws = []
+        for i, (t0, width, share) in enumerate(CHUNKS):
+            raw = keep.tile([P, PACK, width], F32, name=f"raw{i}")
+            nc.sync.dma_start(out=raw[:], in_=tokens[:, :, t0 : t0 + width])
+            raws.append(raw)
+            if i == 0:
+                nc.sync.dma_start(offsets[:], offs)
+
+        nc.vector.memset(warm[:], 0.0)
+        nc.scalar.activation(warmed[:], warm[:], SILU)
+        nc.gpsimd.memset(scales[:], 0)
+        nc.vector.memset(w_bytes[:].rearrange("p e n -> p (e n)").bitcast(I32), 0)
+        nc.vector.memset(placed[:], 0.0)
+
+        for q in range(4):
+            nc.sync.dma_start(
+                out=w_bytes[32 * q : 32 * q + 4, :, :].bitcast(I32),
+                in_=w_scales[:, 0, 4 * q : 4 * q + 4, :].rearrange("e q n -> q e n").bitcast(I32),
+            )
+        nc.sync.dma_start(out=w_codes[:].bitcast(I32), in_=w_words.rearrange("e a p n -> p (e a) n").bitcast(I32))
+        nc.sync.dma_start(out=bias[:], in_=b)
+        nc.sync.dma_start(out=gates[:], in_=gate)
+        nc.sync.dma_start(out=residual[:], in_=xr)
+
+        for i, (t0, width, share) in enumerate(CHUNKS):
+            grouped = keep.tile([P, width, PACK], BF16, name=f"grouped{i}", align_bytes=64)
+            nc.vector.tensor_copy(interleaved(grouped, 0, share), by_rows(raws[i], 0, share))
+            nc.scalar.activation(interleaved(grouped, share, width), by_rows(raws[i], share, width), COPY)
+            nc.vector.quantize_mx(
+                out=words[:, t0 : t0 + width].bitcast(FP8X4),
+                scales=scales[:, t0 : t0 + width],
+                in_=grouped[:].rearrange("p t j -> p (t j)"),
+            )
+
+        results = []
+        for g, experts in enumerate(GROUPS):
+            s0, s1 = experts[0] * C, (experts[-1] + 1) * C
+            listed = offsets[:, s0 // 16 : s1 // 16]
+            slot_words = keep.tile([P, s1 - s0], U32, name=f"slot_words{g}", align_bytes=64)
+            slot_scales = keep.tile([P, s1 - s0], U8, name=f"slot_scales{g}", align_bytes=64)
+            nc.vector.tensor_copy(slot_words[:], words[:].indirect(listed))
+            nc.vector.tensor_copy(slot_scales[:], scales[:].indirect(listed))
+            y = keep.tile([P, s1 - s0], F32, name=f"y{g}")
+            for e in experts:
+                cols = slice(e * C - s0, (e + 1) * C - s0)
+                acc = psum.tile([P, C], F32, name=f"acc{e}")
+                nc.tensor.matmul_mx(
+                    out=acc[:],
+                    lhsT=w_codes[:, e, :].bitcast(FP4X4),
+                    lhsT_scale=w_bytes[:, e, :],
+                    rhs=slot_words[:, cols].bitcast(FP8X4),
+                    rhs_scale=slot_scales[:, cols],
+                    start=True,
+                    stop=True,
+                )
+                nc.scalar.activation(y[:, cols], acc[:], SILU, bias=bias[:, e : e + 1])
+            results.append((s0, s1, y))
+
+        for s0, s1, y in results:
+            nc.vector.tensor_tensor(placed[:].indirect(offsets[:, s0 // 16 : s1 // 16]), y[:], gates[:, s0:s1], MULT)
+
+        for i, (t0, t1) in enumerate(STORES):
+            total = keep.tile([P, t1 - t0], F32, name=f"total{i}")
+            nc.vector.tensor_tensor(total[:], placed[:, t0:t1], residual[:, t0:t1], ADD)
+            queue = nc.sync if i % 2 == 0 else nc.scalar
+            queue.dma_start(out=out[:, t0:t1], in_=total[:])

@@ -18,9 +18,9 @@ COPY = mybir.ActivationFunctionType.Copy
 P = 128
 PACK = 4
 
-CHUNKS = ((0, 512, 320), (512, 512, 320), (1024, 256, 160), (1280, 256, 160))
+CHUNKS = ((0, 512, 256, (512,)), (512, 512, 256, (512,)), (1024, 256, 128, (256,)), (1280, 256, 160, (256,)))
 GROUPS = ((0, 1, 2, 3), (4, 5, 6, 7))
-STORES = ((0, 512), (512, 1024), (1024, 1280), (1280, 1536))
+STORES = ((0, 512), (512, 1024), (1024, 1344), (1344, 1536))
 
 
 def interleaved(grouped, a, b):
@@ -51,12 +51,12 @@ def tile_moe_res_lin_silu_kernel(tc, xT, xr, w_words, w_scales, b, gate, offs, o
 
         tokens = xT.rearrange("(p j) t -> p j t", j=PACK)
         raws = []
-        for i, (t0, width, share) in enumerate(CHUNKS):
+        for i, (t0, width, share, pieces) in enumerate(CHUNKS):
             raw = keep.tile([P, PACK, width], F32, name=f"raw{i}")
             nc.sync.dma_start(out=raw[:], in_=tokens[:, :, t0 : t0 + width])
             raws.append(raw)
-            if i == 0:
-                nc.sync.dma_start(offsets[:], offs)
+
+        nc.sync.dma_start(offsets[:], offs)
 
         nc.vector.memset(warm[:], 0.0)
         nc.scalar.activation(warmed[:], warm[:], SILU)
@@ -74,15 +74,18 @@ def tile_moe_res_lin_silu_kernel(tc, xT, xr, w_words, w_scales, b, gate, offs, o
         nc.sync.dma_start(out=gates[:], in_=gate)
         nc.sync.dma_start(out=residual[:], in_=xr)
 
-        for i, (t0, width, share) in enumerate(CHUNKS):
+        for i, (t0, width, share, pieces) in enumerate(CHUNKS):
             grouped = keep.tile([P, width, PACK], BF16, name=f"grouped{i}", align_bytes=64)
             nc.vector.tensor_copy(interleaved(grouped, 0, share), by_rows(raws[i], 0, share))
             nc.scalar.activation(interleaved(grouped, share, width), by_rows(raws[i], share, width), COPY)
-            nc.vector.quantize_mx(
-                out=words[:, t0 : t0 + width].bitcast(FP8X4),
-                scales=scales[:, t0 : t0 + width],
-                in_=grouped[:].rearrange("p t j -> p (t j)"),
-            )
+            q0 = 0
+            for piece in pieces:
+                nc.vector.quantize_mx(
+                    out=words[:, t0 + q0 : t0 + q0 + piece].bitcast(FP8X4),
+                    scales=scales[:, t0 + q0 : t0 + q0 + piece],
+                    in_=grouped[:, q0 : q0 + piece, :].rearrange("p t j -> p (t j)"),
+                )
+                q0 += piece
 
         results = []
         for g, experts in enumerate(GROUPS):
@@ -114,5 +117,5 @@ def tile_moe_res_lin_silu_kernel(tc, xT, xr, w_words, w_scales, b, gate, offs, o
         for i, (t0, t1) in enumerate(STORES):
             total = keep.tile([P, t1 - t0], F32, name=f"total{i}")
             nc.vector.tensor_tensor(total[:], placed[:, t0:t1], residual[:, t0:t1], ADD)
-            queue = nc.sync if i % 2 == 0 else nc.scalar
+            queue = nc.scalar if i % 2 == 0 else nc.sync
             queue.dma_start(out=out[:, t0:t1], in_=total[:])

@@ -18,7 +18,7 @@ COPY = mybir.ActivationFunctionType.Copy
 P = 128
 PACK = 4
 
-CHUNKS = ((0, 512, 256, (512,)), (512, 512, 256, (512,)), (1024, 256, 128, (256,)), (1280, 256, 160, (256,)))
+CHUNKS = ((0, 768, 384, (512, 256)), (768, 512, 256, (512,)), (1280, 256, 160, (256,)))
 GROUPS = ((0, 1, 2, 3), (4, 5, 6, 7))
 STORES = ((0, 512), (512, 1024), (1024, 1344), (1344, 1536))
 

import concourse.mybir as mybir

K, T, E, C, N = 512, 1536, 8, 128, 128
FLOPS = 2 * K * N * E * C

F32 = mybir.dt.float32
BF16 = mybir.dt.bfloat16
I32 = mybir.dt.int32
U32 = mybir.dt.uint32
U16 = mybir.dt.uint16
U8 = mybir.dt.uint8
FP8X4 = mybir.dt.float8_e4m3fn_x4
FP4X4 = mybir.dt.float4_e2m1fn_x4
MULT, ADD = mybir.AluOpType.mult, mybir.AluOpType.add
SILU = mybir.ActivationFunctionType.Silu
COPY = mybir.ActivationFunctionType.Copy

P = 128
PACK = 4

CHUNKS = ((0, 768, 384, (512, 256)), (768, 512, 256, (512,)), (1280, 256, 160, (256,)))
GROUPS = ((0, 1, 2, 3), (4, 5, 6, 7))
STORES = ((0, 512), (512, 1024), (1024, 1344), (1344, 1536))


def interleaved(grouped, a, b):
    return grouped[:, a:b, :].rearrange("p (c i) t -> p c t i", i=4)


def by_rows(raw, a, b):
    return raw[:, :, a:b].rearrange("p t (c i) -> p c t i", i=4)


def tile_moe_res_lin_silu_kernel(tc, xT, xr, w_words, w_scales, b, gate, offs, out):
    nc = tc.nc
    with (
        tc.tile_pool(name="keep", bufs=1) as keep,
        tc.psum_pool(name="psum", bufs=1) as psum,
    ):
        offsets = keep.tile([P, E * C // 16], U16, name="offsets")
        words = keep.tile([P, T], U32, name="words", align_bytes=64)
        scales = keep.tile([P, T], U8, name="scales", align_bytes=64)
        w_codes = keep.tile([P, E, 2 * N], U8, name="w_codes", align_bytes=64)
        w_bytes = keep.tile([P, E, N], U8, name="w_bytes", align_bytes=64)
        bias = keep.tile([P, E], F32, name="bias")
        gates = keep.tile([P, E * C], F32, name="gates")
        residual = keep.tile([P, T], F32, name="residual")
        placed = keep.tile([P, T], F32, name="placed")
        warm = keep.tile([P, 1], F32, name="warm")
        warmed = keep.tile([P, 1], F32, name="warmed")

        tokens = xT.rearrange("(p j) t -> p j t", j=PACK)
        raws = []
        for i, (t0, width, share, pieces) in enumerate(CHUNKS):
            raw = keep.tile([P, PACK, width], F32, name=f"raw{i}")
            nc.sync.dma_start(out=raw[:], in_=tokens[:, :, t0 : t0 + width])
            raws.append(raw)

        nc.sync.dma_start(offsets[:], offs)

        nc.vector.memset(warm[:], 0.0)
        nc.scalar.activation(warmed[:], warm[:], SILU)
        nc.gpsimd.memset(scales[:], 0)
        nc.vector.memset(w_bytes[:].rearrange("p e n -> p (e n)").bitcast(I32), 0)
        nc.vector.memset(placed[:], 0.0)

        for q in range(4):
            nc.sync.dma_start(
                out=w_bytes[32 * q : 32 * q + 4, :, :].bitcast(I32),
                in_=w_scales[:, 0, 4 * q : 4 * q + 4, :].rearrange("e q n -> q e n").bitcast(I32),
            )
        nc.sync.dma_start(out=w_codes[:].bitcast(I32), in_=w_words.rearrange("e a p n -> p (e a) n").bitcast(I32))
        nc.sync.dma_start(out=bias[:], in_=b)
        nc.sync.dma_start(out=gates[:], in_=gate)
        nc.sync.dma_start(out=residual[:], in_=xr)

        for i, (t0, width, share, pieces) in enumerate(CHUNKS):
            grouped = keep.tile([P, width, PACK], BF16, name=f"grouped{i}", align_bytes=64)
            nc.vector.tensor_copy(interleaved(grouped, 0, share), by_rows(raws[i], 0, share))
            nc.scalar.activation(interleaved(grouped, share, width), by_rows(raws[i], share, width), COPY)
            q0 = 0
            for piece in pieces:
                nc.vector.quantize_mx(
                    out=words[:, t0 + q0 : t0 + q0 + piece].bitcast(FP8X4),
                    scales=scales[:, t0 + q0 : t0 + q0 + piece],
                    in_=grouped[:, q0 : q0 + piece, :].rearrange("p t j -> p (t j)"),
                )
                q0 += piece

        results = []
        for g, experts in enumerate(GROUPS):
            s0, s1 = experts[0] * C, (experts[-1] + 1) * C
            listed = offsets[:, s0 // 16 : s1 // 16]
            slot_words = keep.tile([P, s1 - s0], U32, name=f"slot_words{g}", align_bytes=64)
            slot_scales = keep.tile([P, s1 - s0], U8, name=f"slot_scales{g}", align_bytes=64)
            nc.vector.tensor_copy(slot_words[:], words[:].indirect(listed))
            nc.vector.tensor_copy(slot_scales[:], scales[:].indirect(listed))
            y = keep.tile([P, s1 - s0], F32, name=f"y{g}")
            for e in experts:
                cols = slice(e * C - s0, (e + 1) * C - s0)
                acc = psum.tile([P, C], F32, name=f"acc{e}")
                nc.tensor.matmul_mx(
                    out=acc[:],
                    lhsT=w_codes[:, e, :].bitcast(FP4X4),
                    lhsT_scale=w_bytes[:, e, :],
                    rhs=slot_words[:, cols].bitcast(FP8X4),
                    rhs_scale=slot_scales[:, cols],
                    start=True,
                    stop=True,
                )
                nc.scalar.activation(y[:, cols], acc[:], SILU, bias=bias[:, e : e + 1])
            results.append((s0, s1, y))

        for s0, s1, y in results:
            nc.vector.tensor_tensor(placed[:].indirect(offsets[:, s0 // 16 : s1 // 16]), y[:], gates[:, s0:s1], MULT)

        for i, (t0, t1) in enumerate(STORES):
            total = keep.tile([P, t1 - t0], F32, name=f"total{i}")
            nc.vector.tensor_tensor(total[:], placed[:, t0:t1], residual[:, t0:t1], ADD)
            queue = nc.scalar if i % 2 == 0 else nc.sync
            queue.dma_start(out=out[:, t0:t1], in_=total[:])
